import numpy as np
import ml_dtypes


def mxq(x, axis, fmt="e4m3"):
    dtype, down = {"e4m3": (ml_dtypes.float8_e4m3fn, 7), "e5m2": (ml_dtypes.float8_e5m2, 14)}[fmt]
    v = np.moveaxis(np.asarray(x, np.float32).astype(ml_dtypes.bfloat16).astype(np.float64), axis, -1)
    blocks = v.reshape(v.shape[:-1] + (-1, 32))
    amax = np.abs(blocks).max(-1, keepdims=True)
    byte = np.maximum(np.where(amax > 0, np.frexp(amax)[1] - 1 + 127, 0) - down, 1)
    scale = np.exp2(byte - 127.0)
    codes = (blocks / scale).astype(np.float32).astype(dtype).astype(np.float64)
    return np.moveaxis((codes * scale).reshape(v.shape), -1, axis)


WIDE = False


def mx_kscale(k):
    if not WIDE:
        return np.ones(k)
    levels = np.array([10, -10, 5, -5, 0])
    if k % 512:
        return np.exp2(np.random.permutation(np.resize(levels, k // 32))).repeat(32)
    a = np.empty((k // 512, 16))
    for p in range(k // 512):
        a[p, :8] = np.random.permutation(np.resize(levels, 8))
        for g in range(8):
            far = levels[np.abs(levels - a[p, g]) >= 10]
            a[p, g + 8] = far[np.random.randint(len(far))]
    return np.exp2(a.ravel()).repeat(32)


def f64(x):
    return np.asarray(x).astype(np.float64)


def striped(idx):
    return np.tile(np.asarray(idx).reshape(-1, 16).T, (8, 1)).astype(np.uint16)


def unstriped(offs):
    return offs[:16].T.reshape(-1).astype(np.int64)


E2M1 = np.array([0.0, 0.5, 1.0, 1.5, 2.0, 3.0, 4.0, 6.0, -0.0, -0.5, -1.0, -1.5, -2.0, -3.0, -4.0, -6.0])


def pack_weight(w, fmt):
    k, n = w.shape
    w = f64(np.asarray(w, np.float32).astype(ml_dtypes.bfloat16)).reshape(k // 32, 32, n)
    amax = np.abs(w).max(1)
    if fmt == "e4m3":
        byte = np.frexp(amax)[1] - 1 + 127 - 7
    else:
        mant, ex = np.frexp(amax / 6.0)
        byte = np.where(mant > 0.5, ex, ex - 1) + 127
    byte = np.clip(np.where(amax > 0, byte, 1), 1, 254)
    scaled = (w * np.exp2(127.0 - byte)[:, None, :]).reshape(k, n).astype(np.float32)
    by_word = np.ascontiguousarray(scaled.reshape(k // 512, 128, 4, n).transpose(0, 1, 3, 2))
    if fmt == "e4m3":
        words = by_word.astype(ml_dtypes.float8_e4m3fn).view(np.uint8)
    else:
        c = by_word.astype(ml_dtypes.float4_e2m1fn).view(np.uint8) & 0xF
        words = (c[..., 0::2] | (c[..., 1::2] << 4)).reshape(k // 512, 128, 2 * n)
    return np.ascontiguousarray(words), np.ascontiguousarray(byte.astype(np.uint8).reshape(k // 512, 16, n))


def unpack_weight(words, scales, fmt):
    g, _, n = scales.shape
    words = np.ascontiguousarray(words).reshape(g, 128, n, -1)
    if fmt == "e4m3":
        vals = words.view(ml_dtypes.float8_e4m3fn).astype(np.float64)
    else:
        nib = np.empty((g, 128, n, 4), np.uint8)
        nib[..., 0::2] = words & 0xF
        nib[..., 1::2] = words >> 4
        vals = E2M1[nib]
    vals = vals * np.repeat(np.exp2(scales.astype(np.float64) - 127.0), 8, axis=1)[..., None]
    return vals.transpose(0, 1, 3, 2).reshape(g * 512, n)


B, N, T, D, DV, NQ = 1, 512, 2048, 512, 256, 128


def setup_inputs():
    n = np.random.standard_normal
    idx = np.random.permutation(T)[:B * N]
    s = mx_kscale(D)[:, None]
    u = np.ones(T)
    u[idx] = mx_kscale(B * N)
    r = np.random.uniform(0.5, 2.0, T)
    k = n((D, T)) / s
    v = n((DV, T)) / (u * r)
    kp = pack_weight(k, "e4m3")
    return {
        "qT": (n((B, D, NQ)) * s * (0.60 / np.sqrt(D))).astype(np.float32),
        "k_words": kp[0],
        "k_scales": kp[1],
        "vT": v.astype(np.float32),
        "vs": np.tile(u * r, (128, 1)).astype(np.float32),
        "sink": (2.0 + 3.0 * n((B, NQ, 1))).astype(np.float32),
        "og": n((B, NQ, DV)).astype(np.float32),
        "offs": striped(idx),
    }


def reference(qT, k_words, k_scales, vT, vs, sink, og, offs):
    idx = unstriped(offs)
    k = unpack_weight(k_words, k_scales, "e4m3")
    v = f64(vT)
    pick = lambda x: x[:, idx].reshape(x.shape[0], B, N).transpose(1, 0, 2)
    q = f64(qT)
    score = mxq(q, 1, "e4m3").transpose(0, 2, 1) @ pick(k)
    m = np.maximum(score.max(-1, keepdims=True), f64(sink))
    p = np.exp(score - m)
    total = p.sum(-1, keepdims=True) + np.exp(f64(sink) - m)
    w = p * pick(f64(vs))[:, :1, :]
    y = mxq(w, 2, "e4m3") @ mxq(pick(v).transpose(0, 2, 1), 1, "e4m3")
    y = y / total
    y = y / (1.0 + np.exp(-f64(og)))
    return y

@@ -1,0 +1,168 @@
+from contextlib import ExitStack
+
+import concourse.mybir as mybir
+from concourse.masks import make_identity
+
+F32 = mybir.dt.float32
+BF16 = mybir.dt.bfloat16
+I32 = mybir.dt.int32
+U32 = mybir.dt.uint32
+U16 = mybir.dt.uint16
+U8 = mybir.dt.uint8
+FP8X4 = mybir.dt.float8_e4m3fn_x4
+ALU = mybir.AluOpType
+ACT = mybir.ActivationFunctionType
+
+P = 128
+PACK = 4
+NQ, D, DV, N, T = 128, 512, 256, 512, 2048
+HALF = N // 2
+PER_COL = 16
+
+FLOPS = 2 * NQ * N * (D + DV)
+BYTES = 4 * (D * NQ + P * T + DV * T + T + NQ + 2 * NQ * DV) + 16 * T + 2 * P * (N // PER_COL)
+
+
+def tile_attend_gate_sink_topk_kernel(tc, qT, k_words, k_scales, vT, vs, sink, og, offs, out):
+    nc = tc.nc
+    with ExitStack() as ctx:
+        sb = ctx.enter_context(tc.tile_pool(name="sb", bufs=1))
+        ps = ctx.enter_context(tc.psum_pool(name="ps", bufs=1))
+
+        lst = sb.tile([P, N // PER_COL], U16, name="lst")
+        nc.sync.dma_start(lst[:], offs)
+
+        def slots(first, count):
+            return lst[:, first // PER_COL:(first + count) // PER_COL]
+
+        kscale_pool = sb.tile([P, T], U8, name="kscale_pool", tag="kscales_then_keys", align_bytes=64)
+        vs_pool = sb.tile([P, T], F32, name="vs_pool", tag="vs_then_gate", align_bytes=64)
+        nc.gpsimd.memset(kscale_pool[:].bitcast(I32), 0)
+        nc.vector.memset(vs_pool[:], 0.0)
+
+        q_raw = sb.tile([P, PACK, NQ], F32, name="q_raw", tag="q_then_v1", align_bytes=64)
+        nc.sync.dma_start(q_raw[:], qT[0].rearrange("(p j) q -> p j q", j=PACK))
+        kword_pool = sb.tile([P, T], U32, name="kword_pool", align_bytes=64)
+        nc.sync.dma_start(kword_pool[:].bitcast(I32), k_words[0].rearrange("p t r -> p (t r)").bitcast(I32))
+        sink_col = sb.tile([P, 1], F32, name="sink_col", tag="sink_then_v0", align_bytes=64)
+        nc.scalar.dma_start(sink_col[:], sink[0])
+        for quad in range(4):
+            nc.scalar.dma_start(kscale_pool[32 * quad:32 * quad + 4, :].bitcast(I32),
+                                k_scales[0][4 * quad:4 * quad + 4, :].bitcast(I32))
+        nc.scalar.dma_start(vs_pool[0:1, :], vs[0:1, :])
+        ident = sb.tile([P, P], F32, name="ident")
+        make_identity(nc, ident[:])
+
+        neg_a = sb.tile([P, N + 1], F32, name="neg_a", align_bytes=64)
+        nc.vector.tensor_scalar(out=neg_a[:, N:N + 1], in0=sink_col[:], scalar1=-1.0, scalar2=None, op0=ALU.mult)
+        v_pool0 = sb.tile([P, T], F32, name="v_pool0", tag="sink_then_v0", align_bytes=64)
+        nc.sync.dma_start(v_pool0[:], vT[0:P, :])
+        q_bf = sb.tile([P, NQ, PACK], BF16, name="q_bf", align_bytes=64)
+        nc.vector.tensor_copy(out=q_bf[:], in_=q_raw[:].rearrange("p j q -> p q j"))
+        v_pool1 = sb.tile([P, T], F32, name="v_pool1", tag="q_then_v1", align_bytes=64)
+        nc.sync.dma_start(v_pool1[:], vT[P:2 * P, :])
+        v_pool = [v_pool0, v_pool1]
+        q_codes = sb.tile([P, NQ], U32, name="q_codes", align_bytes=64)
+        q_scales = sb.tile([P, NQ], U8, name="q_scales", align_bytes=64)
+        nc.vector.quantize_mx(out=q_codes[:].bitcast(FP8X4), scales=q_scales[:],
+                              in_=q_bf[:].rearrange("p q j -> p (q j)"))
+
+        k_sc = sb.tile([P, N], U8, name="k_sc", align_bytes=64)
+        nc.vector.tensor_copy(out=k_sc[:], in_=kscale_pool[:].indirect(lst[:]))
+        vs_row = sb.tile([P, N], F32, name="vs_row", align_bytes=64)
+        nc.scalar.activation(out=vs_row[:], in_=vs_pool[:].indirect(lst[:]), func=ACT.Copy)
+        gate_raw = sb.tile([P, DV], F32, name="gate_raw", tag="vs_then_gate", align_bytes=64)
+        nc.sync.dma_start(gate_raw[:], og[0])
+        vs_ps = ps.tile([P, PACK, P], F32, name="vs_ps")
+        for t in range(PACK):
+            nc.tensor.transpose(vs_ps[:, t, :], vs_row[:, t:N:PACK], ident[:])
+        vs_col = sb.tile([P, PACK], F32, name="vs_col")
+        nc.scalar.copy(out=vs_col[:], in_=vs_ps[:, :, 0])
+
+        k_all = sb.tile([P, N], U32, name="k_all", tag="kscales_then_keys", align_bytes=64)
+        k_codes = [k_all[:, h * HALF:(h + 1) * HALF] for h in range(2)]
+        score = [ps.tile([P, HALF], F32, name="score%d" % h) for h in range(2)]
+        for h in range(2):
+            nc.vector.tensor_copy(out=k_codes[h], in_=kword_pool[:].indirect(slots(h * HALF, HALF)))
+            nc.tensor.matmul_mx(out=score[h][:], lhsT=q_codes[:].bitcast(FP8X4), lhsT_scale=q_scales[:],
+                                rhs=k_codes[h].bitcast(FP8X4), rhs_scale=k_sc[:, h * HALF:(h + 1) * HALF],
+                                start=True, stop=True)
+        neg_m = [sb.tile([P, 1], F32, name="neg_m%d" % h) for h in range(2)]
+        dealt = neg_a[:, 0:N].rearrange("q (t s) -> q t s", t=PACK)
+        per_place = HALF // PACK
+        for h in range(2):
+            start = neg_a[:, N:N + 1] if h == 0 else neg_m[0][:]
+            nc.vector.tensor_scalar(out=dealt[:, :, h * per_place:(h + 1) * per_place],
+                                    in0=score[h][:].rearrange("q (s t) -> q t s", t=PACK),
+                                    scalar1=-1.0, scalar2=start, op0=ALU.mult, op1=ALU.min,
+                                    accum_out=neg_m[h][:])
+        prob = sb.tile([P, N + 1], F32, name="prob", align_bytes=64)
+        part_sum = sb.tile([P, 2], F32, name="part_sum")
+        prob_ps = ps.tile([P, PACK, P], F32, name="prob_ps")
+        for h, cols in enumerate((slice(0, HALF), slice(HALF, N + 1))):
+            nc.scalar.activation(out=prob[:, cols], in_=neg_a[:, cols], func=ACT.Exp, bias=neg_m[1][:], scale=-1.0,
+                                 accum_out=part_sum[:, h:h + 1])
+            for t in (2 * h, 2 * h + 1):
+                nc.tensor.transpose(prob_ps[:, t, :], prob[:, t * P:(t + 1) * P], ident[:])
+
+        v_bf = [sb.tile([P, N], BF16, name="v_bf%d" % b, align_bytes=64) for b in range(2)]
+        v_ps = [ps.tile([P, 2, P], F32, name="v_ps%d" % b) for b in range(2)]
+        v_turned = [sb.tile([P, P, PACK], BF16, name="v_turned%d" % b, align_bytes=64) for b in range(2)]
+        v_codes = [sb.tile([P, P], U32, name="v_codes%d" % b, align_bytes=64) for b in range(2)]
+        v_scales = [sb.tile([P, P], U8, name="v_scales%d" % b, align_bytes=64) for b in range(2)]
+
+        def turn_values(b):
+            words = v_bf[b][:].bitcast(F32)
+            for u in range(2):
+                nc.tensor.transpose(v_ps[b][:, u, :], words[:, u:HALF:2], ident[:])
+            nc.scalar.copy(out=v_turned[b][:].rearrange("s e t -> s (e t)").bitcast(F32).rearrange("s (e u) -> s e u", u=2),
+                           in_=v_ps[b][:].rearrange("s u e -> s e u"))
+
+        def quantise_values(b):
+            nc.vector.quantize_mx(out=v_codes[b][:].bitcast(FP8X4), scales=v_scales[b][:],
+                                  in_=v_turned[b][:].rearrange("s e t -> s (e t)"))
+
+        nc.vector.tensor_copy(out=v_bf[0][:], in_=v_pool[0][:].indirect(lst[:]))
+        turn_values(0)
+
+        w_bf = sb.tile([P, NQ, PACK], BF16, name="w_bf", align_bytes=64)
+        nc.vector.tensor_tensor(out=w_bf[:], in0=prob_ps[:].rearrange("s t q -> s q t"),
+                                in1=vs_col[:].unsqueeze(1).to_broadcast([P, NQ, PACK]), op=ALU.mult)
+        quantise_values(0)
+        w_codes = sb.tile([P, NQ], U32, name="w_codes", align_bytes=64)
+        w_scales = sb.tile([P, NQ], U8, name="w_scales", align_bytes=64)
+        nc.vector.quantize_mx(out=w_codes[:].bitcast(FP8X4), scales=w_scales[:],
+                              in_=w_bf[:].rearrange("s q t -> s (q t)"))
+        total = sb.tile([P, 1], F32, name="total")
+        nc.vector.tensor_tensor(out=total[:], in0=part_sum[:, 0:1], in1=part_sum[:, 1:2], op=ALU.add)
+
+        y_ps = [ps.tile([P, P], F32, name="y_ps%d" % b) for b in range(2)]
+
+        def multiply(b):
+            nc.tensor.matmul_mx(out=y_ps[b][:], lhsT=w_codes[:].bitcast(FP8X4), lhsT_scale=w_scales[:],
+                                rhs=v_codes[b][:].bitcast(FP8X4), rhs_scale=v_scales[b][:], start=True, stop=True)
+
+        multiply(0)
+
+        nc.vector.tensor_copy(out=v_bf[1][:, 0:HALF], in_=v_pool[1][:].indirect(slots(0, HALF)))
+        nc.scalar.activation(out=v_bf[1][:, HALF:N], in_=v_pool[1][:].indirect(slots(HALF, HALF)), func=ACT.Copy)
+        inv_total = sb.tile([P, 1], F32, name="inv_total")
+        nc.vector.reciprocal(out=inv_total[:], in_=total[:])
+        gate_tanh = sb.tile([P, DV], F32, name="gate_tanh")
+        nc.scalar.activation(out=gate_tanh[:], in_=gate_raw[:], func=ACT.Tanh, scale=0.5)
+        turn_values(1)
+        factor = sb.tile([P, DV], F32, name="factor")
+        nc.vector.tensor_scalar(out=factor[:], in0=gate_tanh[:], scalar1=1.0, scalar2=inv_total[:],
+                                op0=ALU.add, op1=ALU.mult)
+        result = [sb.tile([P, P], F32, name="result%d" % b) for b in range(2)]
+
+        def finish(b):
+            cols = slice(P * b, P * (b + 1))
+            nc.vector.scalar_tensor_tensor(out=result[b][:], in0=y_ps[b][:], scalar=0.5, in1=factor[:, cols],
+                                           op0=ALU.mult, op1=ALU.mult)
+            nc.sync.dma_start(out[0][:, cols], result[b][:])
+
+        finish(0)
+        quantise_values(1)
+        multiply(1)
+        finish(1)

@@ -1,7 +1,6 @@
 from contextlib import ExitStack
 
 import concourse.mybir as mybir
-from concourse.masks import make_identity
 
 F32 = mybir.dt.float32
 BF16 = mybir.dt.bfloat16
@@ -35,31 +34,35 @@ def tile_attend_gate_sink_topk_kernel(tc, qT, k_words, k_scales, vT, vs, sink, o
         def slots(first, count):
             return lst[:, first // PER_COL:(first + count) // PER_COL]
 
-        kscale_pool = sb.tile([P, T], U8, name="kscale_pool", tag="kscales_then_keys", align_bytes=64)
-        vs_pool = sb.tile([P, T], F32, name="vs_pool", tag="vs_then_gate", align_bytes=64)
-        nc.gpsimd.memset(kscale_pool[:].bitcast(I32), 0)
+        zeros = sb.tile([P, P], F32, name="zeros", align_bytes=64)
+        ident = sb.tile([P, P], F32, name="ident")
+        nc.gpsimd.memset(zeros[:], 0.0)
+        nc.gpsimd.affine_select(out=ident[:], in_=zeros[:], compare_op=ALU.not_equal, fill=1.0, base=0,
+                                pattern=[[-1, P]], channel_multiplier=1)
+
+        kscale_pool = sb.tile([P, T], U8, name="kscale_pool", align_bytes=64)
+        vs_pool = sb.tile([P, T], F32, name="vs_pool", tag="scales_then_prob", align_bytes=64)
+        nc.vector.memset(kscale_pool[:].bitcast(I32), 0)
         nc.vector.memset(vs_pool[:], 0.0)
 
-        q_raw = sb.tile([P, PACK, NQ], F32, name="q_raw", tag="q_then_v1", align_bytes=64)
+        q_raw = sb.tile([P, PACK, NQ], F32, name="q_raw", align_bytes=64)
         nc.sync.dma_start(q_raw[:], qT[0].rearrange("(p j) q -> p j q", j=PACK))
+        for quad in range(4):
+            nc.sync.dma_start(kscale_pool[32 * quad:32 * quad + 4, :].bitcast(I32),
+                              k_scales[0][4 * quad:4 * quad + 4, :].bitcast(I32))
         kword_pool = sb.tile([P, T], U32, name="kword_pool", align_bytes=64)
         nc.sync.dma_start(kword_pool[:].bitcast(I32), k_words[0].rearrange("p t r -> p (t r)").bitcast(I32))
-        sink_col = sb.tile([P, 1], F32, name="sink_col", tag="sink_then_v0", align_bytes=64)
-        nc.scalar.dma_start(sink_col[:], sink[0])
-        for quad in range(4):
-            nc.scalar.dma_start(kscale_pool[32 * quad:32 * quad + 4, :].bitcast(I32),
-                                k_scales[0][4 * quad:4 * quad + 4, :].bitcast(I32))
-        nc.scalar.dma_start(vs_pool[0:1, :], vs[0:1, :])
-        ident = sb.tile([P, P], F32, name="ident")
-        make_identity(nc, ident[:])
+        sink_col = sb.tile([P, 1], F32, name="sink_col", align_bytes=64)
+        nc.sync.dma_start(sink_col[:], sink[0])
+        nc.sync.dma_start(vs_pool[0:1, :], vs[0:1, :])
 
         neg_a = sb.tile([P, N + 1], F32, name="neg_a", align_bytes=64)
-        nc.vector.tensor_scalar(out=neg_a[:, N:N + 1], in0=sink_col[:], scalar1=-1.0, scalar2=None, op0=ALU.mult)
-        v_pool0 = sb.tile([P, T], F32, name="v_pool0", tag="sink_then_v0", align_bytes=64)
-        nc.sync.dma_start(v_pool0[:], vT[0:P, :])
+        nc.scalar.activation(out=neg_a[:, N:N + 1], in_=sink_col[:], func=ACT.Copy, scale=-1.0)
         q_bf = sb.tile([P, NQ, PACK], BF16, name="q_bf", align_bytes=64)
         nc.vector.tensor_copy(out=q_bf[:], in_=q_raw[:].rearrange("p j q -> p q j"))
-        v_pool1 = sb.tile([P, T], F32, name="v_pool1", tag="q_then_v1", align_bytes=64)
+        v_pool0 = sb.tile([P, T], F32, name="v_pool0", align_bytes=64)
+        nc.sync.dma_start(v_pool0[:], vT[0:P, :])
+        v_pool1 = sb.tile([P, T], F32, name="v_pool1", tag="v1_then_w", align_bytes=64)
         nc.sync.dma_start(v_pool1[:], vT[P:2 * P, :])
         v_pool = [v_pool0, v_pool1]
         q_codes = sb.tile([P, NQ], U32, name="q_codes", align_bytes=64)
@@ -71,23 +74,17 @@ def tile_attend_gate_sink_topk_kernel(tc, qT, k_words, k_scales, vT, vs, sink, o
         nc.vector.tensor_copy(out=k_sc[:], in_=kscale_pool[:].indirect(lst[:]))
         vs_row = sb.tile([P, N], F32, name="vs_row", align_bytes=64)
         nc.scalar.activation(out=vs_row[:], in_=vs_pool[:].indirect(lst[:]), func=ACT.Copy)
-        gate_raw = sb.tile([P, DV], F32, name="gate_raw", tag="vs_then_gate", align_bytes=64)
+        gate_raw = sb.tile([P, DV], F32, name="gate_raw", align_bytes=64)
         nc.sync.dma_start(gate_raw[:], og[0])
-        vs_ps = ps.tile([P, PACK, P], F32, name="vs_ps")
-        for t in range(PACK):
-            nc.tensor.transpose(vs_ps[:, t, :], vs_row[:, t:N:PACK], ident[:])
-        vs_col = sb.tile([P, PACK], F32, name="vs_col")
-        nc.scalar.copy(out=vs_col[:], in_=vs_ps[:, :, 0])
 
-        k_all = sb.tile([P, N], U32, name="k_all", tag="kscales_then_keys", align_bytes=64)
-        k_codes = [k_all[:, h * HALF:(h + 1) * HALF] for h in range(2)]
-        score = [ps.tile([P, HALF], F32, name="score%d" % h) for h in range(2)]
+        k_codes = [sb.tile([P, HALF], U32, name="k_codes%d" % h, align_bytes=64) for h in range(2)]
+        score = [ps.tile([P, HALF], F32, name="score%d" % h, tag="score%d" % h) for h in range(2)]
         for h in range(2):
-            nc.vector.tensor_copy(out=k_codes[h], in_=kword_pool[:].indirect(slots(h * HALF, HALF)))
+            nc.vector.tensor_copy(out=k_codes[h][:], in_=kword_pool[:].indirect(slots(h * HALF, HALF)))
             nc.tensor.matmul_mx(out=score[h][:], lhsT=q_codes[:].bitcast(FP8X4), lhsT_scale=q_scales[:],
-                                rhs=k_codes[h].bitcast(FP8X4), rhs_scale=k_sc[:, h * HALF:(h + 1) * HALF],
+                                rhs=k_codes[h][:].bitcast(FP8X4), rhs_scale=k_sc[:, h * HALF:(h + 1) * HALF],
                                 start=True, stop=True)
-        neg_m = [sb.tile([P, 1], F32, name="neg_m%d" % h) for h in range(2)]
+        neg_m = [sb.tile([P, 1], F32, name="neg_m%d" % h, tag="neg_m%d" % h, align_bytes=64) for h in range(2)]
         dealt = neg_a[:, 0:N].rearrange("q (t s) -> q t s", t=PACK)
         per_place = HALF // PACK
         for h in range(2):
@@ -96,7 +93,33 @@ def tile_attend_gate_sink_topk_kernel(tc, qT, k_words, k_scales, vT, vs, sink, o
                                     in0=score[h][:].rearrange("q (s t) -> q t s", t=PACK),
                                     scalar1=-1.0, scalar2=start, op0=ALU.mult, op1=ALU.min,
                                     accum_out=neg_m[h][:])
-        prob = sb.tile([P, N + 1], F32, name="prob", align_bytes=64)
+        vs_ps = ps.tile([P, PACK, P], F32, name="vs_ps", tag="score0")
+        for t in range(PACK):
+            nc.tensor.transpose(vs_ps[:, t, :], vs_row[:, t:N:PACK], ident[:])
+
+        v_bf = [sb.tile([P, N], BF16, name="v_bf0", tag="neg_m0", align_bytes=64),
+                sb.tile([P, N], BF16, name="v_bf1", tag="v1_then_gate", align_bytes=64)]
+        v_ps = [ps.tile([P, 2, P], F32, name="v_ps%d" % b) for b in range(2)]
+
+        def turn_values(b):
+            words = v_bf[b][:].bitcast(F32)
+            for u in range(2):
+                nc.tensor.transpose(v_ps[b][:, u, :], words[:, u:HALF:2], ident[:])
+
+        def interleave_values(b, turned):
+            nc.scalar.copy(out=turned.bitcast(F32).rearrange("s (e u) -> s e u", u=2),
+                           in_=v_ps[b][:].rearrange("s u e -> s e u"))
+
+        def quantise_values(b, turned, tag):
+            codes = sb.tile([P, P], U32, name="v_codes%d" % b, tag=tag, align_bytes=64)
+            scales = sb.tile([P, P], U8, name="v_scales%d" % b, align_bytes=64)
+            nc.vector.quantize_mx(out=codes[:].bitcast(FP8X4), scales=scales[:],
+                                  in_=turned)
+            return codes, scales
+
+        nc.vector.tensor_copy(out=v_bf[0][:], in_=v_pool[0][:].indirect(lst[:]))
+
+        prob = sb.tile([P, N + 1], F32, name="prob", tag="scales_then_prob", align_bytes=64)
         part_sum = sb.tile([P, 2], F32, name="part_sum")
         prob_ps = ps.tile([P, PACK, P], F32, name="prob_ps")
         for h, cols in enumerate((slice(0, HALF), slice(HALF, N + 1))):
@@ -104,65 +127,42 @@ def tile_attend_gate_sink_topk_kernel(tc, qT, k_words, k_scales, vT, vs, sink, o
                                  accum_out=part_sum[:, h:h + 1])
             for t in (2 * h, 2 * h + 1):
                 nc.tensor.transpose(prob_ps[:, t, :], prob[:, t * P:(t + 1) * P], ident[:])
-
-        v_bf = [sb.tile([P, N], BF16, name="v_bf%d" % b, align_bytes=64) for b in range(2)]
-        v_ps = [ps.tile([P, 2, P], F32, name="v_ps%d" % b) for b in range(2)]
-        v_turned = [sb.tile([P, P, PACK], BF16, name="v_turned%d" % b, align_bytes=64) for b in range(2)]
-        v_codes = [sb.tile([P, P], U32, name="v_codes%d" % b, align_bytes=64) for b in range(2)]
-        v_scales = [sb.tile([P, P], U8, name="v_scales%d" % b, align_bytes=64) for b in range(2)]
-
-        def turn_values(b):
-            words = v_bf[b][:].bitcast(F32)
-            for u in range(2):
-                nc.tensor.transpose(v_ps[b][:, u, :], words[:, u:HALF:2], ident[:])
-            nc.scalar.copy(out=v_turned[b][:].rearrange("s e t -> s (e t)").bitcast(F32).rearrange("s (e u) -> s e u", u=2),
-                           in_=v_ps[b][:].rearrange("s u e -> s e u"))
-
-        def quantise_values(b):
-            nc.vector.quantize_mx(out=v_codes[b][:].bitcast(FP8X4), scales=v_scales[b][:],
-                                  in_=v_turned[b][:].rearrange("s e t -> s (e t)"))
-
-        nc.vector.tensor_copy(out=v_bf[0][:], in_=v_pool[0][:].indirect(lst[:]))
+        vs_col = sb.tile([P, PACK], F32, name="vs_col", tag="neg_m1", align_bytes=64)
+        nc.scalar.copy(out=vs_col[:], in_=vs_ps[:, :, 0])
         turn_values(0)
-
-        w_bf = sb.tile([P, NQ, PACK], BF16, name="w_bf", align_bytes=64)
-        nc.vector.tensor_tensor(out=w_bf[:], in0=prob_ps[:].rearrange("s t q -> s q t"),
-                                in1=vs_col[:].unsqueeze(1).to_broadcast([P, NQ, PACK]), op=ALU.mult)
-        quantise_values(0)
-        w_codes = sb.tile([P, NQ], U32, name="w_codes", align_bytes=64)
-        w_scales = sb.tile([P, NQ], U8, name="w_scales", align_bytes=64)
-        nc.vector.quantize_mx(out=w_codes[:].bitcast(FP8X4), scales=w_scales[:],
-                              in_=w_bf[:].rearrange("s q t -> s (q t)"))
         total = sb.tile([P, 1], F32, name="total")
-        nc.vector.tensor_tensor(out=total[:], in0=part_sum[:, 0:1], in1=part_sum[:, 1:2], op=ALU.add)
-
-        y_ps = [ps.tile([P, P], F32, name="y_ps%d" % b) for b in range(2)]
-
-        def multiply(b):
-            nc.tensor.matmul_mx(out=y_ps[b][:], lhsT=w_codes[:].bitcast(FP8X4), lhsT_scale=w_scales[:],
-                                rhs=v_codes[b][:].bitcast(FP8X4), rhs_scale=v_scales[b][:], start=True, stop=True)
-
-        multiply(0)
+        nc.scalar.activation(out=total[:], in_=part_sum[:, 0:1], func=ACT.Identity, bias=part_sum[:, 1:2])
 
         nc.vector.tensor_copy(out=v_bf[1][:, 0:HALF], in_=v_pool[1][:].indirect(slots(0, HALF)))
         nc.scalar.activation(out=v_bf[1][:, HALF:N], in_=v_pool[1][:].indirect(slots(HALF, HALF)), func=ACT.Copy)
-        inv_total = sb.tile([P, 1], F32, name="inv_total")
-        nc.vector.reciprocal(out=inv_total[:], in_=total[:])
+        late = sb.tile([P, 2 * N + 2], BF16, name="late", tag="v1_then_w", align_bytes=64)
+        w_bf, v_turned0, inv_total = late[:, 0:N], late[:, N:2 * N], late[:, 2 * N:2 * N + 2].bitcast(F32)
+        interleave_values(0, v_turned0)
         gate_tanh = sb.tile([P, DV], F32, name="gate_tanh")
         nc.scalar.activation(out=gate_tanh[:], in_=gate_raw[:], func=ACT.Tanh, scale=0.5)
         turn_values(1)
-        factor = sb.tile([P, DV], F32, name="factor")
-        nc.vector.tensor_scalar(out=factor[:], in0=gate_tanh[:], scalar1=1.0, scalar2=inv_total[:],
-                                op0=ALU.add, op1=ALU.mult)
-        result = [sb.tile([P, P], F32, name="result%d" % b) for b in range(2)]
+        v_turned1 = sb.tile([P, N], BF16, name="v_turned1", align_bytes=64)
+        interleave_values(1, v_turned1[:])
+        gate = sb.tile([P, DV], F32, name="gate", tag="v1_then_gate", align_bytes=64)
+        nc.scalar.activation(out=gate[:], in_=gate_tanh[:], func=ACT.Copy, scale=0.5, bias=0.5)
 
-        def finish(b):
+        nc.vector.tensor_tensor(out=w_bf.rearrange("s (q t) -> s q t", t=PACK), in0=prob_ps[:].rearrange("s t q -> s q t"),
+                                in1=vs_col[:].unsqueeze(1).to_broadcast([P, NQ, PACK]), op=ALU.mult)
+        nc.vector.reciprocal(out=inv_total, in_=total[:])
+        v_mx = [quantise_values(0, v_turned0, "neg_m1")]
+        w_codes = sb.tile([P, NQ], U32, name="w_codes", align_bytes=64)
+        w_scales = sb.tile([P, NQ], U8, name="w_scales", align_bytes=64)
+        nc.vector.quantize_mx(out=w_codes[:].bitcast(FP8X4), scales=w_scales[:],
+                              in_=w_bf)
+        v_mx.append(quantise_values(1, v_turned1[:], "v_codes1"))
+
+        for b in range(2):
             cols = slice(P * b, P * (b + 1))
-            nc.vector.scalar_tensor_tensor(out=result[b][:], in0=y_ps[b][:], scalar=0.5, in1=factor[:, cols],
+            codes, scales = v_mx[b]
+            y_ps = ps.tile([P, P], F32, name="y_ps%d" % b)
+            nc.tensor.matmul_mx(out=y_ps[:], lhsT=w_codes[:].bitcast(FP8X4), lhsT_scale=w_scales[:],
+                                rhs=codes[:].bitcast(FP8X4), rhs_scale=scales[:], start=True, stop=True)
+            result = sb.tile([P, P], F32, name="result%d" % b)
+            nc.vector.scalar_tensor_tensor(out=result[:], in0=y_ps[:], scalar=inv_total, in1=gate[:, cols],
                                            op0=ALU.mult, op1=ALU.mult)
-            nc.sync.dma_start(out[0][:, cols], result[b][:])
-
-        finish(0)
-        quantise_values(1)
-        multiply(1)
-        finish(1)
+            nc.sync.dma_start(out[0][:, cols], result[:])

@@ -1,6 +1,7 @@
 from contextlib import ExitStack
 
 import concourse.mybir as mybir
+from concourse.masks import make_identity
 
 F32 = mybir.dt.float32
 BF16 = mybir.dt.bfloat16
@@ -17,6 +18,7 @@ PACK = 4
 NQ, D, DV, N, T = 128, 512, 256, 512, 2048
 HALF = N // 2
 PER_COL = 16
+ROW = 16
 
 FLOPS = 2 * NQ * N * (D + DV)
 BYTES = 4 * (D * NQ + P * T + DV * T + T + NQ + 2 * NQ * DV) + 16 * T + 2 * P * (N // PER_COL)
@@ -34,30 +36,29 @@ def tile_attend_gate_sink_topk_kernel(tc, qT, k_words, k_scales, vT, vs, sink, o
         def slots(first, count):
             return lst[:, first // PER_COL:(first + count) // PER_COL]
 
-        zeros = sb.tile([P, P], F32, name="zeros", align_bytes=64)
-        ident = sb.tile([P, P], F32, name="ident")
-        nc.gpsimd.memset(zeros[:], 0.0)
-        nc.gpsimd.affine_select(out=ident[:], in_=zeros[:], compare_op=ALU.not_equal, fill=1.0, base=0,
-                                pattern=[[-1, P]], channel_multiplier=1)
-
         kscale_pool = sb.tile([P, T], U8, name="kscale_pool", align_bytes=64)
         vs_pool = sb.tile([P, T], F32, name="vs_pool", tag="scales_then_prob", align_bytes=64)
+        sink_rows = sb.tile([P, NQ], F32, name="sink_rows", align_bytes=64)
+        ident = sb.tile([P, P], F32, name="ident")
+        nc.vector.memset(sink_rows[:], 0.0)
         nc.vector.memset(kscale_pool[:].bitcast(I32), 0)
+        nc.vector.memset(ident[:], 0.0)
         nc.vector.memset(vs_pool[:], 0.0)
+        make_identity(nc, ident[:], nomemset=True)
 
         q_raw = sb.tile([P, PACK, NQ], F32, name="q_raw", align_bytes=64)
         nc.sync.dma_start(q_raw[:], qT[0].rearrange("(p j) q -> p j q", j=PACK))
-        for quad in range(4):
-            nc.sync.dma_start(kscale_pool[32 * quad:32 * quad + 4, :].bitcast(I32),
-                              k_scales[0][4 * quad:4 * quad + 4, :].bitcast(I32))
+        nc.sync.dma_start(sink_rows[ROW:ROW + 1, :], sink[0].rearrange("q o -> o q"))
+        for r in range(4):
+            nc.sync.dma_start(kscale_pool[r:P:32, :].bitcast(I32), k_scales[0][r:16:4, :].bitcast(I32))
         kword_pool = sb.tile([P, T], U32, name="kword_pool", align_bytes=64)
         nc.sync.dma_start(kword_pool[:].bitcast(I32), k_words[0].rearrange("p t r -> p (t r)").bitcast(I32))
-        sink_col = sb.tile([P, 1], F32, name="sink_col", align_bytes=64)
-        nc.sync.dma_start(sink_col[:], sink[0])
-        nc.sync.dma_start(vs_pool[0:1, :], vs[0:1, :])
+        nc.sync.dma_start(vs_pool[ROW:ROW + 1, :], vs[0:1, :])
 
         neg_a = sb.tile([P, N + 1], F32, name="neg_a", align_bytes=64)
-        nc.scalar.activation(out=neg_a[:, N:N + 1], in_=sink_col[:], func=ACT.Copy, scale=-1.0)
+        sink_ps = ps.tile([P, P], F32, name="sink_ps")
+        nc.tensor.transpose(sink_ps[:], sink_rows[:], ident[:])
+        nc.scalar.activation(out=neg_a[:, N:N + 1], in_=sink_ps[:, ROW:ROW + 1], func=ACT.Copy, scale=-1.0)
         q_bf = sb.tile([P, NQ, PACK], BF16, name="q_bf", align_bytes=64)
         nc.vector.tensor_copy(out=q_bf[:], in_=q_raw[:].rearrange("p j q -> p q j"))
         v_pool0 = sb.tile([P, T], F32, name="v_pool0", align_bytes=64)
@@ -128,7 +129,7 @@ def tile_attend_gate_sink_topk_kernel(tc, qT, k_words, k_scales, vT, vs, sink, o
             for t in (2 * h, 2 * h + 1):
                 nc.tensor.transpose(prob_ps[:, t, :], prob[:, t * P:(t + 1) * P], ident[:])
         vs_col = sb.tile([P, PACK], F32, name="vs_col", tag="neg_m1", align_bytes=64)
-        nc.scalar.copy(out=vs_col[:], in_=vs_ps[:, :, 0])
+        nc.scalar.copy(out=vs_col[:], in_=vs_ps[:, :, ROW])
         turn_values(0)
         total = sb.tile([P, 1], F32, name="total")
         nc.scalar.activation(out=total[:], in_=part_sum[:, 0:1], func=ACT.Identity, bias=part_sum[:, 1:2])

from contextlib import ExitStack

import concourse.mybir as mybir
from concourse.masks import make_identity

F32 = mybir.dt.float32
BF16 = mybir.dt.bfloat16
I32 = mybir.dt.int32
U32 = mybir.dt.uint32
U16 = mybir.dt.uint16
U8 = mybir.dt.uint8
FP8X4 = mybir.dt.float8_e4m3fn_x4
ALU = mybir.AluOpType
ACT = mybir.ActivationFunctionType

P = 128
PACK = 4
NQ, D, DV, N, T = 128, 512, 256, 512, 2048
HALF = N // 2
PER_COL = 16
ROW = 16

FLOPS = 2 * NQ * N * (D + DV)
BYTES = 4 * (D * NQ + P * T + DV * T + T + NQ + 2 * NQ * DV) + 16 * T + 2 * P * (N // PER_COL)


def tile_attend_gate_sink_topk_kernel(tc, qT, k_words, k_scales, vT, vs, sink, og, offs, out):
    nc = tc.nc
    with ExitStack() as ctx:
        sb = ctx.enter_context(tc.tile_pool(name="sb", bufs=1))
        ps = ctx.enter_context(tc.psum_pool(name="ps", bufs=1))

        lst = sb.tile([P, N // PER_COL], U16, name="lst")
        nc.sync.dma_start(lst[:], offs)

        def slots(first, count):
            return lst[:, first // PER_COL:(first + count) // PER_COL]

        kscale_pool = sb.tile([P, T], U8, name="kscale_pool", align_bytes=64)
        vs_pool = sb.tile([P, T], F32, name="vs_pool", tag="scales_then_prob", align_bytes=64)
        sink_rows = sb.tile([P, NQ], F32, name="sink_rows", align_bytes=64)
        ident = sb.tile([P, P], F32, name="ident")
        nc.vector.memset(sink_rows[:], 0.0)
        nc.vector.memset(kscale_pool[:].bitcast(I32), 0)
        nc.vector.memset(ident[:], 0.0)
        nc.vector.memset(vs_pool[:], 0.0)
        make_identity(nc, ident[:], nomemset=True)

        q_raw = sb.tile([P, PACK, NQ], F32, name="q_raw", align_bytes=64)
        nc.sync.dma_start(q_raw[:], qT[0].rearrange("(p j) q -> p j q", j=PACK))
        nc.sync.dma_start(sink_rows[ROW:ROW + 1, :], sink[0].rearrange("q o -> o q"))
        for r in range(4):
            nc.sync.dma_start(kscale_pool[r:P:32, :].bitcast(I32), k_scales[0][r:16:4, :].bitcast(I32))
        kword_pool = sb.tile([P, T], U32, name="kword_pool", align_bytes=64)
        nc.sync.dma_start(kword_pool[:].bitcast(I32), k_words[0].rearrange("p t r -> p (t r)").bitcast(I32))
        nc.sync.dma_start(vs_pool[ROW:ROW + 1, :], vs[0:1, :])

        neg_a = sb.tile([P, N + 1], F32, name="neg_a", align_bytes=64)
        sink_ps = ps.tile([P, P], F32, name="sink_ps")
        nc.tensor.transpose(sink_ps[:], sink_rows[:], ident[:])
        nc.scalar.activation(out=neg_a[:, N:N + 1], in_=sink_ps[:, ROW:ROW + 1], func=ACT.Copy, scale=-1.0)
        q_bf = sb.tile([P, NQ, PACK], BF16, name="q_bf", align_bytes=64)
        nc.vector.tensor_copy(out=q_bf[:], in_=q_raw[:].rearrange("p j q -> p q j"))
        v_pool0 = sb.tile([P, T], F32, name="v_pool0", align_bytes=64)
        nc.sync.dma_start(v_pool0[:], vT[0:P, :])
        v_pool1 = sb.tile([P, T], F32, name="v_pool1", tag="v1_then_w", align_bytes=64)
        nc.sync.dma_start(v_pool1[:], vT[P:2 * P, :])
        v_pool = [v_pool0, v_pool1]
        q_codes = sb.tile([P, NQ], U32, name="q_codes", align_bytes=64)
        q_scales = sb.tile([P, NQ], U8, name="q_scales", align_bytes=64)
        nc.vector.quantize_mx(out=q_codes[:].bitcast(FP8X4), scales=q_scales[:],
                              in_=q_bf[:].rearrange("p q j -> p (q j)"))

        k_sc = sb.tile([P, N], U8, name="k_sc", align_bytes=64)
        nc.vector.tensor_copy(out=k_sc[:], in_=kscale_pool[:].indirect(lst[:]))
        vs_row = sb.tile([P, N], F32, name="vs_row", align_bytes=64)
        nc.scalar.activation(out=vs_row[:], in_=vs_pool[:].indirect(lst[:]), func=ACT.Copy)
        gate_raw = sb.tile([P, DV], F32, name="gate_raw", align_bytes=64)
        nc.sync.dma_start(gate_raw[:], og[0])

        k_codes = [sb.tile([P, HALF], U32, name="k_codes%d" % h, align_bytes=64) for h in range(2)]
        score = [ps.tile([P, HALF], F32, name="score%d" % h, tag="score%d" % h) for h in range(2)]
        for h in range(2):
            nc.vector.tensor_copy(out=k_codes[h][:], in_=kword_pool[:].indirect(slots(h * HALF, HALF)))
            nc.tensor.matmul_mx(out=score[h][:], lhsT=q_codes[:].bitcast(FP8X4), lhsT_scale=q_scales[:],
                                rhs=k_codes[h][:].bitcast(FP8X4), rhs_scale=k_sc[:, h * HALF:(h + 1) * HALF],
                                start=True, stop=True)
        neg_m = [sb.tile([P, 1], F32, name="neg_m%d" % h, tag="neg_m%d" % h, align_bytes=64) for h in range(2)]
        dealt = neg_a[:, 0:N].rearrange("q (t s) -> q t s", t=PACK)
        per_place = HALF // PACK
        for h in range(2):
            start = neg_a[:, N:N + 1] if h == 0 else neg_m[0][:]
            nc.vector.tensor_scalar(out=dealt[:, :, h * per_place:(h + 1) * per_place],
                                    in0=score[h][:].rearrange("q (s t) -> q t s", t=PACK),
                                    scalar1=-1.0, scalar2=start, op0=ALU.mult, op1=ALU.min,
                                    accum_out=neg_m[h][:])
        vs_ps = ps.tile([P, PACK, P], F32, name="vs_ps", tag="score0")
        for t in range(PACK):
            nc.tensor.transpose(vs_ps[:, t, :], vs_row[:, t:N:PACK], ident[:])

        v_bf = [sb.tile([P, N], BF16, name="v_bf0", tag="neg_m0", align_bytes=64),
                sb.tile([P, N], BF16, name="v_bf1", tag="v1_then_gate", align_bytes=64)]
        v_ps = [ps.tile([P, 2, P], F32, name="v_ps%d" % b) for b in range(2)]

        def turn_values(b):
            words = v_bf[b][:].bitcast(F32)
            for u in range(2):
                nc.tensor.transpose(v_ps[b][:, u, :], words[:, u:HALF:2], ident[:])

        def interleave_values(b, turned):
            nc.scalar.copy(out=turned.bitcast(F32).rearrange("s (e u) -> s e u", u=2),
                           in_=v_ps[b][:].rearrange("s u e -> s e u"))

        def quantise_values(b, turned, tag):
            codes = sb.tile([P, P], U32, name="v_codes%d" % b, tag=tag, align_bytes=64)
            scales = sb.tile([P, P], U8, name="v_scales%d" % b, align_bytes=64)
            nc.vector.quantize_mx(out=codes[:].bitcast(FP8X4), scales=scales[:],
                                  in_=turned)
            return codes, scales

        nc.vector.tensor_copy(out=v_bf[0][:], in_=v_pool[0][:].indirect(lst[:]))

        prob = sb.tile([P, N + 1], F32, name="prob", tag="scales_then_prob", align_bytes=64)
        part_sum = sb.tile([P, 2], F32, name="part_sum")
        prob_ps = ps.tile([P, PACK, P], F32, name="prob_ps")
        for h, cols in enumerate((slice(0, HALF), slice(HALF, N + 1))):
            nc.scalar.activation(out=prob[:, cols], in_=neg_a[:, cols], func=ACT.Exp, bias=neg_m[1][:], scale=-1.0,
                                 accum_out=part_sum[:, h:h + 1])
            for t in (2 * h, 2 * h + 1):
                nc.tensor.transpose(prob_ps[:, t, :], prob[:, t * P:(t + 1) * P], ident[:])
        vs_col = sb.tile([P, PACK], F32, name="vs_col", tag="neg_m1", align_bytes=64)
        nc.scalar.copy(out=vs_col[:], in_=vs_ps[:, :, ROW])
        turn_values(0)
        total = sb.tile([P, 1], F32, name="total")
        nc.scalar.activation(out=total[:], in_=part_sum[:, 0:1], func=ACT.Identity, bias=part_sum[:, 1:2])

        nc.vector.tensor_copy(out=v_bf[1][:, 0:HALF], in_=v_pool[1][:].indirect(slots(0, HALF)))
        nc.scalar.activation(out=v_bf[1][:, HALF:N], in_=v_pool[1][:].indirect(slots(HALF, HALF)), func=ACT.Copy)
        late = sb.tile([P, 2 * N + 2], BF16, name="late", tag="v1_then_w", align_bytes=64)
        w_bf, v_turned0, inv_total = late[:, 0:N], late[:, N:2 * N], late[:, 2 * N:2 * N + 2].bitcast(F32)
        interleave_values(0, v_turned0)
        gate_tanh = sb.tile([P, DV], F32, name="gate_tanh")
        nc.scalar.activation(out=gate_tanh[:], in_=gate_raw[:], func=ACT.Tanh, scale=0.5)
        turn_values(1)
        v_turned1 = sb.tile([P, N], BF16, name="v_turned1", align_bytes=64)
        interleave_values(1, v_turned1[:])
        gate = sb.tile([P, DV], F32, name="gate", tag="v1_then_gate", align_bytes=64)
        nc.scalar.activation(out=gate[:], in_=gate_tanh[:], func=ACT.Copy, scale=0.5, bias=0.5)

        nc.vector.tensor_tensor(out=w_bf.rearrange("s (q t) -> s q t", t=PACK), in0=prob_ps[:].rearrange("s t q -> s q t"),
                                in1=vs_col[:].unsqueeze(1).to_broadcast([P, NQ, PACK]), op=ALU.mult)
        nc.vector.reciprocal(out=inv_total, in_=total[:])
        v_mx = [quantise_values(0, v_turned0, "neg_m1")]
        w_codes = sb.tile([P, NQ], U32, name="w_codes", align_bytes=64)
        w_scales = sb.tile([P, NQ], U8, name="w_scales", align_bytes=64)
        nc.vector.quantize_mx(out=w_codes[:].bitcast(FP8X4), scales=w_scales[:],
                              in_=w_bf)
        v_mx.append(quantise_values(1, v_turned1[:], "v_codes1"))

        for b in range(2):
            cols = slice(P * b, P * (b + 1))
            codes, scales = v_mx[b]
            y_ps = ps.tile([P, P], F32, name="y_ps%d" % b)
            nc.tensor.matmul_mx(out=y_ps[:], lhsT=w_codes[:].bitcast(FP8X4), lhsT_scale=w_scales[:],
                                rhs=codes[:].bitcast(FP8X4), rhs_scale=scales[:], start=True, stop=True)
            result = sb.tile([P, P], F32, name="result%d" % b)
            nc.vector.scalar_tensor_tensor(out=result[:], in0=y_ps[:], scalar=inv_total, in1=gate[:, cols],
                                           op0=ALU.mult, op1=ALU.mult)
            nc.sync.dma_start(out[0][:, cols], result[:])
